import numpy as np, ml_dtypes
CORES = [17,57,65,89,97,121]
N = 6
import mx_ref
NC = 128
CNT = [[0,6,0,8,0,114],[8,0,0,94,26,0],[40,12,0,20,56,0],[6,20,94,0,6,2],[20,90,0,6,0,12],[54,0,34,0,40,0]]
OFF = [[sum(c[:e]) for e in range(N + 1)] for c in CNT]
BF = ml_dtypes.bfloat16
def setup_inputs(rng):
    def f(*shape):
        return mx_ref.flush((rng.standard_normal(shape, dtype=np.float32) * np.exp2(rng.integers(-2, 3, shape[:-1] + (1,)))).astype(BF))
    return {"w": f(N, 128, 512), "x": f(N, 128, 4 * NC)}
def setup_inputs_blocks(rng):
    d = setup_inputs(rng)
    for k in ("w", "x"): d[k] = mx_ref.spread(d[k], rng, 4)
    return d
def setup_inputs_wide(rng):
    d = setup_inputs(rng)
    for k in ("w", "x"): d[k] = mx_ref.flush((d[k].astype(np.float32) * np.exp2(rng.integers(-8, 9, (N, 1, 1))).astype(np.float32)).astype(BF))
    return d
def setup_inputs_zeros(rng):
    d = setup_inputs(rng); v = d["x"].reshape(N, 128, -1, 4).copy()
    v[np.broadcast_to((rng.random((N, 1, v.shape[2], 1)) < 0.33), v.shape)] = 0
    d["x"] = v.reshape(d["x"].shape)
    return d
def reference(w, x):
    y = np.zeros((N, 128, NC), np.float32)
    for e in range(N):
        t = np.concatenate([x[j][:, 4 * OFF[j][e]:4 * OFF[j][e + 1]] for j in range(N)], axis=1)
        y[e] = mx_ref.matmul(mx_ref.quantize(w[e]), mx_ref.quantize(t))
    return {"y": y}

@@ -1,0 +1,132 @@
+from concourse.bass import DstId, RemoteDMATransfer
+from concourse.mybir import dt
+
+SCRATCH = {
+    "xt": ("sbuf", [128, 512], "bfloat16"),
+    "wt": ("sbuf", [128, 512], "bfloat16"),
+    "xq": ("sbuf", [128, 128], "float8_e4m3fn_x4"),
+    "xs": ("sbuf", [128, 128], "uint8"),
+    "wq": ("sbuf", [128, 128], "float8_e4m3fn_x4"),
+    "ws": ("sbuf", [128, 128], "uint8"),
+    "bq": ("sbuf", [128, 128], "float8_e4m3fn_x4"),
+    "bs": ("sbuf", [128, 128], "uint8"),
+    "acc": ("psum", [128, 512], "float32"),
+    "yt": ("sbuf", [128, 128], "float32"),
+}
+SEMAPHORES = ["ldx", "ldw", "qx", "qw", "fed", "arrived", "sent", "mm", "cp", "st"]
+
+FEED_ENGINES = 4
+OUT_ENGINES = 8
+CODES, SCALES = 0, 1
+
+
+def _engines(mask, k, skip=0):
+    bits = [b for b in range(mask.bit_length()) if (mask >> b) & 1]
+    m = 0
+    for b in bits[skip:skip + k]:
+        m |= 1 << b
+    return m
+
+
+def _plan(T, topo):
+    cores = list(T.cores)
+    cnt = T.tables["CNT"]
+    n = len(cores)
+    cols = sum(cnt[0])
+    off = [[sum(cnt[j][:e]) for e in range(n)] for j in range(n)]
+    pos = [[sum(cnt[i][e] for i in range(j)) for e in range(n)] for j in range(n)]
+    feeds, direct, helper = {}, {}, {}
+    expect = [0] * n
+    for j, src in enumerate(cores):
+        dests = sorted([e for e in range(n) if cnt[j][e] > 0], key=lambda e: -cnt[j][e])
+        direct[j] = [e for e in dests if topo.may_write(src, cores[e])]
+        far = [e for e in dests if not topo.may_write(src, cores[e])]
+        for e in dests:
+            expect[e] += 2 * OUT_ENGINES
+        feeds[j] = []
+        if not far:
+            continue
+        near = [c for c in range(topo.CHIPS * topo.CORES_PER_CHIP)
+                if topo.chip(c) == topo.chip(src) and c not in cores
+                and all(topo.may_write(c, cores[e]) for e in far)]
+        near.sort(key=lambda c: (topo.die(c) != topo.die(src), c))
+        groups = [g for g in (far[:1], far[1:]) if g]
+        hull = [(min(off[j][e] for e in g), max(off[j][e] + cnt[j][e] for e in g)) for g in groups]
+        width = max(hi - lo for lo, hi in hull)
+        for kind in (CODES, SCALES):
+            call = []
+            for i, g in enumerate(groups):
+                h = near[kind * len(groups) + i]
+                lo = min(hull[i][0], cols - width)
+                call.append((h, lo, lo + width))
+                helper[h] = (kind, j, g)
+            feeds[j].append((kind, call))
+    return {"cores": cores, "cnt": cnt, "off": off, "pos": pos, "feeds": feeds, "direct": direct,
+            "helper": helper, "expect": expect}
+
+
+def _view(buf, kind, a, b):
+    v = buf[:, a:b]
+    return v.bitcast(dt.uint8) if kind == CODES else v
+
+
+def _deliver(g, T, topo, P, me, j, e, kind):
+    dst = P["cores"][e]
+    rid, pid, _ = topo.addr(dst)
+    a, p, k = P["off"][j][e], P["pos"][j][e], P["cnt"][j][e]
+    g.remote_dma(out_ap=_view((T.bq, T.bs)[kind], kind, p, p + k),
+                 in_ap=_view((T.xq, T.xs)[kind], kind, a, a + k),
+                 remote_sem=T.sem.arrived, local_sem=T.sem.sent, pid=pid, routing_id=rid,
+                 dma_engine_mask=_engines(topo.mask(me, dst), OUT_ENGINES))
+    return OUT_ENGINES
+
+
+def rank_program(g, core, T, topo):
+    P = _plan(T, topo)
+
+    if core in P["helper"]:
+        kind, j, group = P["helper"][core]
+        g.wait_ge(T.sem.fed, FEED_ENGINES)
+        left = 0
+        for e in group:
+            left += _deliver(g, T, topo, P, core, j, e, kind)
+        g.wait_ge(T.sem.sent, left)
+        return
+
+    j = T.rank_of(core)
+    if j is None:
+        return
+
+    g.sync.dma_start(T.xt[:], T.x[:]).then_inc(T.sem.ldx, 16)
+    g.scalar.dma_start(T.wt[:], T.w[:]).then_inc(T.sem.ldw, 16)
+    g.vector.wait_ge(T.sem.ldx, 16)
+    g.vector.quantize_mx(T.xq[:], T.xs[:], T.xt[:]).then_inc(T.sem.qx, 1)
+    g.vector.wait_ge(T.sem.ldw, 16)
+    g.vector.quantize_mx(T.wq[:], T.ws[:], T.wt[:]).then_inc(T.sem.qw, 1)
+
+    g.wait_ge(T.sem.qx, 1)
+    left = 0
+    for kind, call in P["feeds"][j]:
+        transfers = []
+        for i, (h, a, b) in enumerate(call):
+            rid, pid, _ = topo.addr(h)
+            buf = (T.xq, T.xs)[kind]
+            transfers.append(RemoteDMATransfer(
+                dst_ids=[DstId(rid=rid, pnc=pid)],
+                dma_engine_mask=_engines(topo.mask(core, h), FEED_ENGINES, i * FEED_ENGINES),
+                remote_sem=T.sem.fed, src=_view(buf, kind, a, b), dst=_view(buf, kind, a, b)))
+            left += FEED_ENGINES
+        g.remote_dma_fused(transfers, local_sem=T.sem.sent)
+    for e in P["direct"][j]:
+        for kind in (CODES, SCALES):
+            left += _deliver(g, T, topo, P, core, j, e, kind)
+
+    g.tensor.wait_ge(T.sem.qw, 1)
+    g.tensor.wait_ge(T.sem.arrived, P["expect"][j])
+    g.tensor.matmul_mx(T.acc[:, 0:128], T.wq[:], T.ws[:], T.bq[:], T.bs[:], True, True).then_inc(T.sem.mm, 1)
+    g.vector.wait_ge(T.sem.mm, 1)
+    g.vector.tensor_copy(T.yt[:], T.acc[:, 0:128]).then_inc(T.sem.cp, 1)
+    g.sync.wait_ge(T.sem.cp, 1)
+    g.sync.dma_start(T.y[:], T.yt[:]).then_inc(T.sem.st, 16)
+    g.sync.wait_ge(T.sem.st, 16)
+    g.wait_ge(T.sem.sent, left)

@@ -13,10 +13,12 @@ SCRATCH = {
     "acc": ("psum", [128, 512], "float32"),
     "yt": ("sbuf", [128, 128], "float32"),
 }
-SEMAPHORES = ["ldx", "ldw", "qx", "qw", "fed", "arrived", "sent", "mm", "cp", "st"]
+SEMAPHORES = ["ldx", "ldw", "qx", "qw", "fedp", "fedc", "arrived", "sent", "mm", "cp", "st"]
 
 FEED_ENGINES = 4
+LONG_ENGINES = 8
 OUT_ENGINES = 8
+SPLIT = 48
 CODES, SCALES = 0, 1
 
 
@@ -32,37 +34,54 @@ def _plan(T, topo):
     cores = list(T.cores)
     cnt = T.tables["CNT"]
     n = len(cores)
-    cols = sum(cnt[0])
     off = [[sum(cnt[j][:e]) for e in range(n)] for j in range(n)]
     pos = [[sum(cnt[i][e] for i in range(j)) for e in range(n)] for j in range(n)]
-    feeds, direct, helper = {}, {}, {}
+    own, free, pieces = {}, {}, {}
     expect = [0] * n
+    leave, arrive = {}, {}
     for j, src in enumerate(cores):
-        dests = sorted([e for e in range(n) if cnt[j][e] > 0], key=lambda e: -cnt[j][e])
-        direct[j] = [e for e in dests if topo.may_write(src, cores[e])]
-        far = [e for e in dests if not topo.may_write(src, cores[e])]
-        for e in dests:
+        dests = [e for e in range(n) if cnt[j][e] > 0]
+        mine = [(cnt[j][e], e, off[j][e]) for e in dests if topo.may_write(src, cores[e])]
+        ps = [(cnt[j][e], e, off[j][e]) for e in dests if not topo.may_write(src, cores[e])]
+        free[j] = [c for c in range(topo.CHIPS * topo.CORES_PER_CHIP)
+                   if topo.chip(c) == topo.chip(src) and c not in cores]
+        slots = bin(topo.mask(src, free[j][0])).count("1") // FEED_ENGINES
+        while len(ps) < slots and max(ps + mine)[0] > SPLIT:
+            big = max(ps + mine)
+            k, e, a = big
+            rest, half = (k - k // 2, e, a), (k // 2, e, a + k - k // 2)
+            if big in mine:
+                mine.remove(big)
+                mine.append(rest)
+                ps.append(half)
+            else:
+                ps.remove(big)
+                ps += [rest, half]
+        ps.sort(key=lambda p: (-p[0], p[1], p[2]))
+        mine.sort(key=lambda p: (-p[0], p[1], p[2]))
+        pieces[j], own[j] = ps, mine
+        for k, e, a in ps + mine:
             expect[e] += 2 * OUT_ENGINES
-        feeds[j] = []
-        if not far:
-            continue
-        near = [c for c in range(topo.CHIPS * topo.CORES_PER_CHIP)
-                if topo.chip(c) == topo.chip(src) and c not in cores
-                and all(topo.may_write(c, cores[e]) for e in far)]
-        near.sort(key=lambda c: (topo.die(c) != topo.die(src), c))
-        groups = [g for g in (far[:1], far[1:]) if g]
-        hull = [(min(off[j][e] for e in g), max(off[j][e] + cnt[j][e] for e in g)) for g in groups]
-        width = max(hi - lo for lo, hi in hull)
-        for kind in (CODES, SCALES):
-            call = []
-            for i, g in enumerate(groups):
-                h = near[kind * len(groups) + i]
-                lo = min(hull[i][0], cols - width)
-                call.append((h, lo, lo + width))
-                helper[h] = (kind, j, g)
-            feeds[j].append((kind, call))
-    return {"cores": cores, "cnt": cnt, "off": off, "pos": pos, "feeds": feeds, "direct": direct,
-            "helper": helper, "expect": expect}
+        for k, e, a in mine:
+            d = topo.die(src)
+            leave[(j, False, d)] = leave.get((j, False, d), 0) + k
+            arrive[(e, d)] = arrive.get((e, d), 0) + k
+    helper, serves = {}, {}
+    for k, j, e, a in sorted([(-k, j, e, a) for j in range(n) for k, e, a in pieces[j]]):
+        isfar = not topo.may_write(cores[j], cores[e])
+        h = min([c for c in free[j] if topo.may_write(c, cores[e])],
+                key=lambda c: (max(leave.get((j, isfar, topo.die(c)), 0), arrive.get((e, topo.die(c)), 0)),
+                               sum(1 for x in cores if topo.may_write(c, x)),
+                               topo.die(c) != topo.die(cores[j]), c))
+        free[j].remove(h)
+        d = topo.die(h)
+        leave[(j, isfar, d)] = leave.get((j, isfar, d), 0) - k
+        arrive[(e, d)] = arrive.get((e, d), 0) - k
+        fed = LONG_ENGINES if pieces[j].index((-k, e, a)) < 2 else FEED_ENGINES
+        helper[h] = (j, e, a, -k, fed)
+        serves[(j, e, a)] = h
+    return {"cores": cores, "cnt": cnt, "off": off, "pos": pos, "pieces": pieces, "own": own,
+            "helper": helper, "serves": serves, "expect": expect, "leave": leave, "arrive": arrive}
 
 
 def _view(buf, kind, a, b):
@@ -70,10 +89,10 @@ def _view(buf, kind, a, b):
     return v.bitcast(dt.uint8) if kind == CODES else v
 
 
-def _deliver(g, T, topo, P, me, j, e, kind):
+def _deliver(g, T, topo, P, me, j, e, a, k, kind):
     dst = P["cores"][e]
     rid, pid, _ = topo.addr(dst)
-    a, p, k = P["off"][j][e], P["pos"][j][e], P["cnt"][j][e]
+    p = P["pos"][j][e] + a - P["off"][j][e]
     g.remote_dma(out_ap=_view((T.bq, T.bs)[kind], kind, p, p + k),
                  in_ap=_view((T.xq, T.xs)[kind], kind, a, a + k),
                  remote_sem=T.sem.arrived, local_sem=T.sem.sent, pid=pid, routing_id=rid,
@@ -81,15 +100,33 @@ def _deliver(g, T, topo, P, me, j, e, kind):
     return OUT_ENGINES
 
 
+def _feed(g, T, topo, P, me, j, kind, items):
+    cols = sum(P["cnt"][j])
+    width = max(p[0] for p, _, _ in items)
+    buf = (T.xq, T.xs)[kind]
+    transfers, left = [], 0
+    for (k, e, a), eng, skip in items:
+        h = P["serves"][(j, e, a)]
+        rid, pid, _ = topo.addr(h)
+        lo = min(a, cols - width)
+        transfers.append(RemoteDMATransfer(
+            dst_ids=[DstId(rid=rid, pnc=pid)], dma_engine_mask=_engines(topo.mask(me, h), eng, skip),
+            remote_sem=(T.sem.fedc, T.sem.fedp)[kind],
+            src=_view(buf, kind, lo, lo + width), dst=_view(buf, kind, lo, lo + width)))
+        left += eng
+    g.remote_dma_fused(transfers, local_sem=T.sem.sent)
+    return left
+
+
 def rank_program(g, core, T, topo):
     P = _plan(T, topo)
 
     if core in P["helper"]:
-        kind, j, group = P["helper"][core]
-        g.wait_ge(T.sem.fed, FEED_ENGINES)
-        left = 0
-        for e in group:
-            left += _deliver(g, T, topo, P, core, j, e, kind)
+        j, e, a, k, fed = P["helper"][core]
+        g.wait_ge(T.sem.fedp, FEED_ENGINES)
+        left = _deliver(g, T, topo, P, core, j, e, a, k, SCALES)
+        g.wait_ge(T.sem.fedc, fed)
+        left += _deliver(g, T, topo, P, core, j, e, a, k, CODES)
         g.wait_ge(T.sem.sent, left)
         return
 
@@ -106,20 +143,16 @@ def rank_program(g, core, T, topo):
 
     g.wait_ge(T.sem.qx, 1)
     left = 0
-    for kind, call in P["feeds"][j]:
-        transfers = []
-        for i, (h, a, b) in enumerate(call):
-            rid, pid, _ = topo.addr(h)
-            buf = (T.xq, T.xs)[kind]
-            transfers.append(RemoteDMATransfer(
-                dst_ids=[DstId(rid=rid, pnc=pid)],
-                dma_engine_mask=_engines(topo.mask(core, h), FEED_ENGINES, i * FEED_ENGINES),
-                remote_sem=T.sem.fed, src=_view(buf, kind, a, b), dst=_view(buf, kind, a, b)))
-            left += FEED_ENGINES
-        g.remote_dma_fused(transfers, local_sem=T.sem.sent)
-    for e in P["direct"][j]:
-        for kind in (CODES, SCALES):
-            left += _deliver(g, T, topo, P, core, j, e, kind)
+    ps = P["pieces"][j]
+    if ps:
+        left += _feed(g, T, topo, P, core, j, SCALES, [(p, FEED_ENGINES, i * FEED_ENGINES) for i, p in enumerate(ps)])
+        left += _feed(g, T, topo, P, core, j, CODES, [(p, LONG_ENGINES, i * LONG_ENGINES) for i, p in enumerate(ps[:2])])
+        if ps[2:]:
+            left += _feed(g, T, topo, P, core, j, CODES,
+                          [(p, FEED_ENGINES, (2 + i) * FEED_ENGINES) for i, p in enumerate(ps[2:])])
+    for k, e, a in P["own"][j]:
+        for kind in (SCALES, CODES):
+            left += _deliver(g, T, topo, P, core, j, e, a, k, kind)
 
     g.tensor.wait_ge(T.sem.qw, 1)
     g.tensor.wait_ge(T.sem.arrived, P["expect"][j])

from concourse.bass import DstId, RemoteDMATransfer
from concourse.mybir import dt

SCRATCH = {
    "xt": ("sbuf", [128, 512], "bfloat16"),
    "wt": ("sbuf", [128, 512], "bfloat16"),
    "xq": ("sbuf", [128, 128], "float8_e4m3fn_x4"),
    "xs": ("sbuf", [128, 128], "uint8"),
    "wq": ("sbuf", [128, 128], "float8_e4m3fn_x4"),
    "ws": ("sbuf", [128, 128], "uint8"),
    "bq": ("sbuf", [128, 128], "float8_e4m3fn_x4"),
    "bs": ("sbuf", [128, 128], "uint8"),
    "acc": ("psum", [128, 512], "float32"),
    "yt": ("sbuf", [128, 128], "float32"),
}
SEMAPHORES = ["ldx", "ldw", "qx", "qw", "fedp", "fedc", "arrived", "sent", "mm", "cp", "st"]

FEED_ENGINES = 4
LONG_ENGINES = 8
OUT_ENGINES = 8
SPLIT = 48
CODES, SCALES = 0, 1


def _engines(mask, k, skip=0):
    bits = [b for b in range(mask.bit_length()) if (mask >> b) & 1]
    m = 0
    for b in bits[skip:skip + k]:
        m |= 1 << b
    return m


def _plan(T, topo):
    cores = list(T.cores)
    cnt = T.tables["CNT"]
    n = len(cores)
    off = [[sum(cnt[j][:e]) for e in range(n)] for j in range(n)]
    pos = [[sum(cnt[i][e] for i in range(j)) for e in range(n)] for j in range(n)]
    own, free, pieces = {}, {}, {}
    expect = [0] * n
    leave, arrive = {}, {}
    for j, src in enumerate(cores):
        dests = [e for e in range(n) if cnt[j][e] > 0]
        mine = [(cnt[j][e], e, off[j][e]) for e in dests if topo.may_write(src, cores[e])]
        ps = [(cnt[j][e], e, off[j][e]) for e in dests if not topo.may_write(src, cores[e])]
        free[j] = [c for c in range(topo.CHIPS * topo.CORES_PER_CHIP)
                   if topo.chip(c) == topo.chip(src) and c not in cores]
        slots = bin(topo.mask(src, free[j][0])).count("1") // FEED_ENGINES
        while len(ps) < slots and max(ps + mine)[0] > SPLIT:
            big = max(ps + mine)
            k, e, a = big
            rest, half = (k - k // 2, e, a), (k // 2, e, a + k - k // 2)
            if big in mine:
                mine.remove(big)
                mine.append(rest)
                ps.append(half)
            else:
                ps.remove(big)
                ps += [rest, half]
        ps.sort(key=lambda p: (-p[0], p[1], p[2]))
        mine.sort(key=lambda p: (-p[0], p[1], p[2]))
        pieces[j], own[j] = ps, mine
        for k, e, a in ps + mine:
            expect[e] += 2 * OUT_ENGINES
        for k, e, a in mine:
            d = topo.die(src)
            leave[(j, False, d)] = leave.get((j, False, d), 0) + k
            arrive[(e, d)] = arrive.get((e, d), 0) + k
    helper, serves = {}, {}
    for k, j, e, a in sorted([(-k, j, e, a) for j in range(n) for k, e, a in pieces[j]]):
        isfar = not topo.may_write(cores[j], cores[e])
        h = min([c for c in free[j] if topo.may_write(c, cores[e])],
                key=lambda c: (max(leave.get((j, isfar, topo.die(c)), 0), arrive.get((e, topo.die(c)), 0)),
                               sum(1 for x in cores if topo.may_write(c, x)),
                               topo.die(c) != topo.die(cores[j]), c))
        free[j].remove(h)
        d = topo.die(h)
        leave[(j, isfar, d)] = leave.get((j, isfar, d), 0) - k
        arrive[(e, d)] = arrive.get((e, d), 0) - k
        fed = LONG_ENGINES if pieces[j].index((-k, e, a)) < 2 else FEED_ENGINES
        helper[h] = (j, e, a, -k, fed)
        serves[(j, e, a)] = h
    return {"cores": cores, "cnt": cnt, "off": off, "pos": pos, "pieces": pieces, "own": own,
            "helper": helper, "serves": serves, "expect": expect, "leave": leave, "arrive": arrive}


def _view(buf, kind, a, b):
    v = buf[:, a:b]
    return v.bitcast(dt.uint8) if kind == CODES else v


def _deliver(g, T, topo, P, me, j, e, a, k, kind):
    dst = P["cores"][e]
    rid, pid, _ = topo.addr(dst)
    p = P["pos"][j][e] + a - P["off"][j][e]
    g.remote_dma(out_ap=_view((T.bq, T.bs)[kind], kind, p, p + k),
                 in_ap=_view((T.xq, T.xs)[kind], kind, a, a + k),
                 remote_sem=T.sem.arrived, local_sem=T.sem.sent, pid=pid, routing_id=rid,
                 dma_engine_mask=_engines(topo.mask(me, dst), OUT_ENGINES))
    return OUT_ENGINES


def _feed(g, T, topo, P, me, j, kind, items):
    cols = sum(P["cnt"][j])
    width = max(p[0] for p, _, _ in items)
    buf = (T.xq, T.xs)[kind]
    transfers, left = [], 0
    for (k, e, a), eng, skip in items:
        h = P["serves"][(j, e, a)]
        rid, pid, _ = topo.addr(h)
        lo = min(a, cols - width)
        transfers.append(RemoteDMATransfer(
            dst_ids=[DstId(rid=rid, pnc=pid)], dma_engine_mask=_engines(topo.mask(me, h), eng, skip),
            remote_sem=(T.sem.fedc, T.sem.fedp)[kind],
            src=_view(buf, kind, lo, lo + width), dst=_view(buf, kind, lo, lo + width)))
        left += eng
    g.remote_dma_fused(transfers, local_sem=T.sem.sent)
    return left


def rank_program(g, core, T, topo):
    P = _plan(T, topo)

    if core in P["helper"]:
        j, e, a, k, fed = P["helper"][core]
        g.wait_ge(T.sem.fedp, FEED_ENGINES)
        left = _deliver(g, T, topo, P, core, j, e, a, k, SCALES)
        g.wait_ge(T.sem.fedc, fed)
        left += _deliver(g, T, topo, P, core, j, e, a, k, CODES)
        g.wait_ge(T.sem.sent, left)
        return

    j = T.rank_of(core)
    if j is None:
        return

    g.sync.dma_start(T.xt[:], T.x[:]).then_inc(T.sem.ldx, 16)
    g.scalar.dma_start(T.wt[:], T.w[:]).then_inc(T.sem.ldw, 16)
    g.vector.wait_ge(T.sem.ldx, 16)
    g.vector.quantize_mx(T.xq[:], T.xs[:], T.xt[:]).then_inc(T.sem.qx, 1)
    g.vector.wait_ge(T.sem.ldw, 16)
    g.vector.quantize_mx(T.wq[:], T.ws[:], T.wt[:]).then_inc(T.sem.qw, 1)

    g.wait_ge(T.sem.qx, 1)
    left = 0
    ps = P["pieces"][j]
    if ps:
        left += _feed(g, T, topo, P, core, j, SCALES, [(p, FEED_ENGINES, i * FEED_ENGINES) for i, p in enumerate(ps)])
        left += _feed(g, T, topo, P, core, j, CODES, [(p, LONG_ENGINES, i * LONG_ENGINES) for i, p in enumerate(ps[:2])])
        if ps[2:]:
            left += _feed(g, T, topo, P, core, j, CODES,
                          [(p, FEED_ENGINES, (2 + i) * FEED_ENGINES) for i, p in enumerate(ps[2:])])
    for k, e, a in P["own"][j]:
        for kind in (SCALES, CODES):
            left += _deliver(g, T, topo, P, core, j, e, a, k, kind)

    g.tensor.wait_ge(T.sem.qw, 1)
    g.tensor.wait_ge(T.sem.arrived, P["expect"][j])
    g.tensor.matmul_mx(T.acc[:, 0:128], T.wq[:], T.ws[:], T.bq[:], T.bs[:], True, True).then_inc(T.sem.mm, 1)
    g.vector.wait_ge(T.sem.mm, 1)
    g.vector.tensor_copy(T.yt[:], T.acc[:, 0:128]).then_inc(T.sem.cp, 1)
    g.sync.wait_ge(T.sem.cp, 1)
    g.sync.dma_start(T.y[:], T.yt[:]).then_inc(T.sem.st, 16)
    g.sync.wait_ge(T.sem.st, 16)
    g.wait_ge(T.sem.sent, left)
